import numpy as np
import ml_dtypes


def mxq(x, axis, fmt="e4m3"):
    dtype, down = {"e4m3": (ml_dtypes.float8_e4m3fn, 7), "e5m2": (ml_dtypes.float8_e5m2, 14)}[fmt]
    v = np.moveaxis(np.asarray(x, np.float32).astype(ml_dtypes.bfloat16).astype(np.float64), axis, -1)
    blocks = v.reshape(v.shape[:-1] + (-1, 32))
    amax = np.abs(blocks).max(-1, keepdims=True)
    byte = np.maximum(np.where(amax > 0, np.frexp(amax)[1] - 1 + 127, 0) - down, 1)
    scale = np.exp2(byte - 127.0)
    codes = (blocks / scale).astype(np.float32).astype(dtype).astype(np.float64)
    return np.moveaxis((codes * scale).reshape(v.shape), -1, axis)


WIDE = False


def mx_kscale(k):
    if not WIDE:
        return np.ones(k)
    levels = np.array([10, -10, 5, -5, 0])
    if k % 512:
        return np.exp2(np.random.permutation(np.resize(levels, k // 32))).repeat(32)
    a = np.empty((k // 512, 16))
    for p in range(k // 512):
        a[p, :8] = np.random.permutation(np.resize(levels, 8))
        for g in range(8):
            far = levels[np.abs(levels - a[p, g]) >= 10]
            a[p, g + 8] = far[np.random.randint(len(far))]
    return np.exp2(a.ravel()).repeat(32)


def f64(x):
    return np.asarray(x).astype(np.float64)


def striped(idx):
    return np.tile(idx.reshape(-1, 16).T, (8, 1)).astype(np.uint16)


def unstriped(offs):
    return offs[:16].T.reshape(-1).astype(np.int64)


def striped8(idx):
    return np.concatenate([x.reshape(-1, 16).T for x in idx]).astype(np.uint16)


def runs(offs, k):
    lists = np.stack([offs[16 * r : 16 * r + 16].T.reshape(-1) for r in range(8)]).astype(np.int64)
    return lists[np.arange(k) % 512 // 64]


def pack_weight(w):
    k, n = w.shape
    w = f64(np.asarray(w, np.float32).astype(ml_dtypes.bfloat16)).reshape(k // 32, 32, n)
    amax = np.abs(w).max(1)
    byte = np.clip(np.where(amax > 0, np.frexp(amax)[1] - 1 + 127 - 7, 1), 1, 254)
    scaled = (w * np.exp2(127.0 - byte)[:, None, :]).reshape(k, n).astype(np.float32)
    words = np.ascontiguousarray(scaled.reshape(k // 512, 128, 4, n).transpose(0, 1, 3, 2)).astype(ml_dtypes.float8_e4m3fn).view(np.uint8)
    return words, np.ascontiguousarray(byte.astype(np.uint8).reshape(k // 512, 16, n))


def unpack_weight(words, scales):
    g, p, n, _ = words.shape
    vals = np.ascontiguousarray(words).view(ml_dtypes.float8_e4m3fn).astype(np.float64) * np.repeat(np.exp2(scales.astype(np.float64) - 127.0), 8, axis=1)[..., None]
    return vals.transpose(0, 1, 3, 2).reshape(g * 512, n)

def planes(y):
    n, m = y.shape
    v = y.astype(np.float32).astype(ml_dtypes.bfloat16).astype(np.float64).reshape(n // 32, 32, m)
    top = np.abs(v).max(1)
    byte = np.clip(np.where(top > 0, np.frexp(top)[1] - 1 + 127 - 7, 1), 1, 254)
    codes = (v * np.exp2(127.0 - byte)[:, None, :]).reshape(n, m).astype(np.float32).astype(ml_dtypes.float8_e4m3fn).view(np.uint8)
    words = codes.reshape(n // 512, 128, 4, m).transpose(0, 1, 3, 2)
    return np.ascontiguousarray(words), np.ascontiguousarray(byte.astype(np.uint8).reshape(n // 512, 16, m))


K, T, S, N, G, H = 512, 2048, 512, 512, 2048, 512


def setup_inputs():
    n = np.random.standard_normal
    s = mx_kscale(K)[:, None]
    u = mx_kscale(S)
    packed_xT = pack_weight(n((K, T)) * s)
    packed_dT = pack_weight(n((K, G)) / s)
    packed_w1 = pack_weight(n((H, N)) / np.sqrt(2 * H) / u[:, None])
    packed_w2 = pack_weight(n((K, N)) / np.sqrt(2 * K) / s)
    return {
        "x_words": packed_xT[0],
        "x_scales": packed_xT[1],
        "d_words": packed_dT[0],
        "d_scales": packed_dT[1],
        "gn": (np.random.uniform(0.5, 1.5, (H, 1)) * u[:, None]).astype(np.float32),
        "w1_words": packed_w1[0],
        "w1_scales": packed_w1[1],
        "w2_words": packed_w2[0],
        "w2_scales": packed_w2[1],
        "offs": striped(np.random.permutation(T)[:S]),
        "k1": striped8(np.random.randint(0, G, (8, H))),
        "n1": striped(np.random.permutation(S)),
        "n2": striped(np.random.permutation(S)),
        "two": striped(np.random.permutation(T)[:S]),
        "n3": striped(np.random.permutation(S)),
        "n4": striped(np.random.permutation(S)),
    }


def reference(x_words, x_scales, d_words, d_scales, gn, w1_words, w1_scales, w2_words, w2_scales, offs, k1, n1, n2, two, n3, n4):
    d_k1 = unpack_weight(d_words, d_scales)[np.arange(K)[:, None], runs(k1, K)]
    xq = unpack_weight(x_words, x_scales)[:, unstriped(offs)]
    s = 0.0625 * (d_k1.T @ xq)
    ex = np.exp(s)
    z = f64(gn) * (np.log(ex + ex[:, unstriped(n1)]) - s[:, unstriped(n2)])
    x_two = unpack_weight(x_words, x_scales)[:, unstriped(two)]
    h = unpack_weight(w1_words, w1_scales).T @ mxq(z, 0, "e4m3") + unpack_weight(w2_words, w2_scales).T @ x_two
    st = h + 0.5 * h[:, unstriped(n3)]
    out_0 = st - st[:, unstriped(n4)]
    return (out_0,) + planes(out_0)

@@ -1,0 +1,236 @@
+from contextlib import ExitStack
+
+import concourse.mybir as mybir
+
+F32 = mybir.dt.float32
+BF16 = mybir.dt.bfloat16
+I32 = mybir.dt.int32
+U32 = mybir.dt.uint32
+U16 = mybir.dt.uint16
+U8 = mybir.dt.uint8
+FP8X4 = mybir.dt.float8_e4m3fn_x4
+ACT = mybir.ActivationFunctionType
+ALU = mybir.AluOpType
+
+P = 128
+PACK = 4
+TABLE = 2048
+S = 512
+HALF = S // 2
+PAD = 16
+FLOPS = 3 * 2 * 512 * 512 * 512
+
+
+def tile_picked_kmixlsehop_none_po_kernel(
+    tc, x_words, x_scales, d_words, d_scales, gn, w1_words, w1_scales, w2_words, w2_scales,
+    offs, k1, n1, n2, two, n3, n4, out_0, out_1, out_2,
+):
+    nc = tc.nc
+
+    def words_of(dram):
+        return dram[0].rearrange("p n t -> p (n t)").bitcast(I32)
+
+    def half_of(lst, a):
+        return lst[:, a * (HALF // 16) : (a + 1) * (HALF // 16)]
+
+    def cols(a):
+        return slice(a * HALF, (a + 1) * HALF)
+
+    def block(t):
+        return slice(t * P, (t + 1) * P)
+
+    def deal_words(copy, dst, src):
+        copy(out=dst.rearrange("p (t c i) -> p c t i", t=PACK, i=4), in_=src.rearrange("p (c i t) -> p c t i", t=PACK, i=4))
+
+    def deal_bytes(dst, src):
+        nc.vector.tensor_copy(out=dst.rearrange("p (t m) -> p t m", t=PACK), in_=src.rearrange("p (m t) -> p t m", t=PACK))
+
+    def weave(dst, src):
+        nc.vector.tensor_copy(out=dst.rearrange("p (c i) t -> p c t i", i=4), in_=src.rearrange("p t (c i) -> p c t i", i=4))
+
+    with ExitStack() as ctx:
+        lists = ctx.enter_context(tc.tile_pool(name="lists", bufs=1))
+        sb = ctx.enter_context(tc.tile_pool(name="sb", bufs=1))
+        ps = ctx.enter_context(tc.psum_pool(name="ps", bufs=1))
+
+        def load_list(dram, name):
+            tl = lists.tile([P, S // 16], U16, name=name)
+            nc.sync.dma_start(tl[:], dram)
+            return tl
+
+        def new(shape, dtype, name, tag=""):
+            return sb.tile(shape, dtype, name=name, tag=tag or name, align_bytes=64)
+
+        l_k1 = load_list(k1, "l_k1")
+        ds_tab = new([P, TABLE], U8, "ds_tab", tag="scales")
+        nc.sync.dma_start(ds_tab[:].bitcast(I32), d_scales[0].bitcast(I32).unsqueeze(1).to_broadcast([16, 8, TABLE // 4]))
+        l_offs = load_list(offs, "l_offs")
+        xs_tab = new([P, TABLE], U8, "xs_tab")
+        for q in range(4):
+            rows = x_scales[0, 4 * q : 4 * q + 4, :].bitcast(I32)
+            nc.sync.dma_start(xs_tab[32 * q : 32 * q + 32, :].bitcast(I32), rows.unsqueeze(0).to_broadcast([8, 4, TABLE // 4]))
+        dw_tab = new([P, TABLE], U32, "dw_tab", tag="table")
+        nc.sync.dma_start(dw_tab[:].bitcast(I32), words_of(d_words))
+        gain = new([P, PACK], F32, "gain")
+        nc.sync.dma_start(gain[:], gn.rearrange("(p t) o -> p (t o)", t=PACK))
+        l_two = load_list(two, "l_two")
+        l_n1 = load_list(n1, "l_n1")
+        xw_tab = new([P, TABLE], U32, "xw_tab")
+        nc.sync.dma_start(xw_tab[:].bitcast(I32), words_of(x_words))
+        l_n2 = load_list(n2, "l_n2")
+        l_n3 = load_list(n3, "l_n3")
+        l_n4 = load_list(n4, "l_n4")
+
+        key_plane = new([P, S], U8, "key_plane")
+        nc.vector.memset(key_plane[:].bitcast(I32), 0)
+        ex_win = [new([P, S + PAD], F32, f"ex_win{t}") for t in range(PACK)]
+        hh_win = [new([P, S + PAD], F32, f"hh_win{t}") for t in range(PACK)]
+        for win in ex_win + hh_win:
+            nc.vector.memset(win[:, S:], 0.0)
+
+        ds_got = new([P, S], U8, "ds_got")
+        nc.vector.tensor_copy(out=ds_got[:], in_=ds_tab[:].indirect(l_k1[:]))
+        ds_dealt = new([P, S], U8, "ds_dealt")
+        deal_bytes(ds_dealt[:], ds_got[:])
+        for q in range(4):
+            nc.scalar.dma_start(key_plane[32 * q : 32 * q + 4, :].bitcast(I32), ds_dealt[32 * q : 32 * q + 32 : 8, :].bitcast(I32))
+        tok_plane = new([P, S], U8, "tok_plane", tag="scales")
+        nc.vector.tensor_copy(out=tok_plane[:], in_=xs_tab[:].indirect(l_offs[:]))
+        dw_got = new([P, S], U32, "dw_got", tag="ds_got")
+        nc.vector.tensor_copy(out=dw_got[:], in_=dw_tab[:].indirect(l_k1[:]))
+        key_words = new([P, S], U32, "key_words")
+        deal_words(nc.vector.tensor_copy, key_words[:], dw_got[:])
+        tok_words = new([P, S], U32, "tok_words")
+        nc.vector.tensor_copy(out=tok_words[:], in_=xw_tab[:].indirect(l_offs[:]))
+
+        w_raw = new([P, 2, S], U32, "w_raw", tag="table")
+        w_dealt = new([P, 2, S], U32, "w_dealt")
+        for w, words in enumerate((w1_words, w2_words)):
+            nc.sync.dma_start(w_raw[:, w, :].bitcast(I32), words_of(words))
+
+        score = [ps.tile([P, S], F32, name=f"score{t}", tag=f"bank{t}") for t in range(PACK)]
+        for t in range(PACK):
+            nc.tensor.matmul_mx(
+                out=score[t][:], lhsT=key_words[:, block(t)].bitcast(FP8X4), lhsT_scale=key_plane[:, block(t)],
+                rhs=tok_words[:].bitcast(FP8X4), rhs_scale=tok_plane[:], start=True, stop=True,
+            )
+        for t in range(PACK):
+            nc.scalar.activation(out=ex_win[t][:, :S], in_=score[t][:], func=ACT.Exp, scale=0.0625)
+
+        neg_gain = new([P, PACK], F32, "neg_gain")
+        nc.vector.tensor_scalar(out=neg_gain[:], in0=gain[:], scalar1=-0.0625, scalar2=None, op0=ALU.mult)
+        two_words = new([P, S], U32, "two_words")
+        nc.vector.tensor_copy(out=two_words[:], in_=xw_tab[:].indirect(l_two[:]))
+        two_plane = new([P, S], U8, "two_plane", tag="scales")
+        nc.vector.tensor_copy(out=two_plane[:], in_=xs_tab[:].indirect(l_two[:]))
+        ws_raw = new([P, S], U8, "ws_raw", tag="xs_tab")
+        nc.vector.memset(ws_raw[:].bitcast(I32), 0)
+        for w, scales in enumerate((w1_scales, w2_scales)):
+            for q in range(4):
+                nc.sync.dma_start(
+                    ws_raw[32 * q + 4 * w : 32 * q + 4 * w + 4, :].bitcast(I32), scales[0, 4 * q : 4 * q + 4, :].bitcast(I32)
+                )
+
+
+        gs_win = [new([P, S], F32, f"gs_win{t}") for t in range(PACK)]
+        for t in range(PACK):
+            nc.scalar.activation(out=gs_win[t][:], in_=score[t][:], func=ACT.Copy, scale=neg_gain[:, t : t + 1])
+
+        ex = [new([P, S], F32, f"ex{t}") for t in range(PACK)]
+        pair = [new([P, S], F32, f"pair{t}") for t in range(PACK)]
+        for t in range(PACK):
+            nc.vector.tensor_copy(out=ex[t][:], in_=ex_win[t][:, :S])
+            if t > 0:
+                nc.vector.tensor_tensor(out=pair[t - 1][:], in0=ex_win[t - 1][:].indirect(l_n1[:]), in1=ex[t - 1][:], op=ALU.add)
+        nc.vector.tensor_tensor(out=pair[3][:], in0=ex_win[3][:].indirect(l_n1[:]), in1=ex[3][:], op=ALU.add)
+
+        for w in range(2):
+            deal_words(nc.vector.tensor_copy, w_dealt[:, w, :], w_raw[:, w, :])
+        w_plane = new([P, S], U8, "w_plane")
+        deal_bytes(w_plane[:], ws_raw[:])
+
+        def project_two(bank, t, a):
+            nc.tensor.matmul_mx(
+                out=bank[:], lhsT=w_dealt[:, 1, block(t)].bitcast(FP8X4), lhsT_scale=w_plane[4:P, block(t)],
+                rhs=two_words[:, cols(a)].bitcast(FP8X4), rhs_scale=two_plane[:, cols(a)], start=True, stop=False,
+            )
+
+        hbank = [[ps.tile([P, HALF], F32, name=f"h{a}_{t}", tag=f"bank{4 * (1 - a) + t}") for t in range(PACK)] for a in range(2)]
+        for a in range(2):
+            for t in range(PACK):
+                project_two(hbank[a][t], t, a)
+
+        lse = [new([P, S], F32, f"lse{t}") for t in range(PACK)]
+        gs_got = [[new([P, HALF], F32, f"gs_got{a}_{t}") for t in range(PACK)] for a in range(2)]
+        z_rows = [new([P, PACK, HALF], BF16, f"z_rows{a}") for a in range(2)]
+
+        def fetch_gs(a, t):
+            nc.scalar.activation(out=gs_got[a][t][:], in_=gs_win[t][:].indirect(half_of(l_n2, a)), func=ACT.Copy)
+
+        def make_z(a, t):
+            nc.vector.scalar_tensor_tensor(
+                out=z_rows[a][:, t, :], in0=lse[t][:, cols(a)], scalar=gain[:, t : t + 1], in1=gs_got[a][t][:],
+                op0=ALU.mult, op1=ALU.add,
+            )
+
+        h_sb = [new([P, S], F32, f"h_sb{t}") for t in range(PACK)]
+
+        def second_product(a):
+            z_woven = new([P, HALF, PACK], BF16, f"z_woven{a}")
+            weave(z_woven[:], z_rows[a][:])
+            z_words = new([P, HALF], U32, f"z_words{a}")
+            z_plane = new([P, HALF], U8, f"z_plane{a}")
+            nc.vector.quantize_mx(out=z_words[:].bitcast(FP8X4), scales=z_plane[:], in_=z_woven[:].rearrange("p j t -> p (j t)"))
+            for t in range(PACK):
+                nc.tensor.matmul_mx(
+                    out=hbank[a][t][:], lhsT=w_dealt[:, 0, block(t)].bitcast(FP8X4), lhsT_scale=w_plane[:, block(t)],
+                    rhs=z_words[:].bitcast(FP8X4), rhs_scale=z_plane[:], start=False, stop=True,
+                )
+
+        def empty_h(a, t):
+            nc.scalar.activation(out=hh_win[t][:, cols(a)], in_=hbank[a][t][:], func=ACT.Copy, scale=0.5)
+            nc.scalar.copy(out=h_sb[t][:, cols(a)], in_=hbank[a][t][:])
+
+        for t in range(PACK):
+            nc.scalar.activation(out=lse[t][:], in_=pair[t][:], func=ACT.Ln)
+            fetch_gs(0, t)
+            make_z(0, t)
+        for t in range(PACK):
+            fetch_gs(1, t)
+        second_product(0)
+        for t in range(PACK):
+            make_z(1, t)
+        second_product(1)
+        for t in range(PACK):
+            empty_h(0, t)
+
+        st = [new([P, S], F32, f"st{t}") for t in range(PACK)]
+        st_got = [[new([P, HALF], F32, f"st_got{a}_{t}") for t in range(PACK)] for a in range(2)]
+        y = [new([P, PACK, HALF], F32, f"y{a}") for a in range(2)]
+        y_rows = out_0.rearrange("(p t) j -> p t j", t=PACK)
+        y_plane = new([P, S], U8, "y_plane")
+
+        def hop(a, t):
+            nc.scalar.activation(out=st_got[a][t][:], in_=st[t][:].indirect(half_of(l_n4, a)), func=ACT.Copy)
+            nc.vector.tensor_tensor(out=y[a][:, t, :], in0=st[t][:, cols(a)], in1=st_got[a][t][:], op=ALU.subtract)
+            nc.sync.dma_start(y_rows[:, t, cols(a)], y[a][:, t, :])
+
+        def planes(a):
+            y_woven = new([P, HALF, PACK], BF16, f"y_woven{a}")
+            weave(y_woven[:], y[a][:])
+            y_words = new([P, HALF], U32, f"y_words{a}")
+            nc.vector.quantize_mx(out=y_words[:].bitcast(FP8X4), scales=y_plane[:, cols(a)], in_=y_woven[:].rearrange("p j t -> p (j t)"))
+            nc.sync.dma_start(words_of(out_1)[:, cols(a)], y_words[:].bitcast(I32))
+
+        for t in range(PACK):
+            empty_h(1, t)
+            nc.vector.tensor_tensor(out=st[t][:], in0=hh_win[t][:].indirect(l_n3[:]), in1=h_sb[t][:], op=ALU.add)
+        for t in range(PACK):
+            hop(0, t)
+        planes(0)
+        for t in range(PACK):
+            hop(1, t)
+        planes(1)
+        for q in range(4):
+            queue = nc.scalar if q % 2 else nc.sync
+            queue.dma_start(out_2[0, 4 * q : 4 * q + 4, :].bitcast(I32), y_plane[32 * q : 32 * q + 4, :].bitcast(I32))

@@ -45,12 +45,13 @@ def tile_picked_kmixlsehop_none_po_kernel(
     def deal_bytes(dst, src):
         nc.vector.tensor_copy(out=dst.rearrange("p (t m) -> p t m", t=PACK), in_=src.rearrange("p (m t) -> p t m", t=PACK))
 
-    def weave(dst, src):
-        nc.vector.tensor_copy(out=dst.rearrange("p (c i) t -> p c t i", i=4), in_=src.rearrange("p t (c i) -> p c t i", i=4))
+    def weave(copy, dst, src):
+        copy(out=dst.rearrange("p (c i) t -> p c t i", i=4), in_=src.rearrange("p t (c i) -> p c t i", i=4))
 
     with ExitStack() as ctx:
         lists = ctx.enter_context(tc.tile_pool(name="lists", bufs=1))
         sb = ctx.enter_context(tc.tile_pool(name="sb", bufs=1))
+        reuse = ctx.enter_context(tc.tile_pool(name="reuse", bufs=1))
         ps = ctx.enter_context(tc.psum_pool(name="ps", bufs=1))
 
         def load_list(dram, name):
@@ -61,31 +62,41 @@ def tile_picked_kmixlsehop_none_po_kernel(
         def new(shape, dtype, name, tag=""):
             return sb.tile(shape, dtype, name=name, tag=tag or name, align_bytes=64)
 
-        l_k1 = load_list(k1, "l_k1")
         ds_tab = new([P, TABLE], U8, "ds_tab", tag="scales")
+        xs_tab = new([P, TABLE], U8, "xs_tab")
+        nc.vector.memset(xs_tab[:].bitcast(I32), 0)
+        l_k1 = load_list(k1, "l_k1")
         nc.sync.dma_start(ds_tab[:].bitcast(I32), d_scales[0].bitcast(I32).unsqueeze(1).to_broadcast([16, 8, TABLE // 4]))
         l_offs = load_list(offs, "l_offs")
-        xs_tab = new([P, TABLE], U8, "xs_tab")
         for q in range(4):
-            rows = x_scales[0, 4 * q : 4 * q + 4, :].bitcast(I32)
-            nc.sync.dma_start(xs_tab[32 * q : 32 * q + 32, :].bitcast(I32), rows.unsqueeze(0).to_broadcast([8, 4, TABLE // 4]))
+            nc.scalar.dma_start(xs_tab[32 * q : 32 * q + 4, :].bitcast(I32), x_scales[0, 4 * q : 4 * q + 4, :].bitcast(I32))
         dw_tab = new([P, TABLE], U32, "dw_tab", tag="table")
         nc.sync.dma_start(dw_tab[:].bitcast(I32), words_of(d_words))
-        gain = new([P, PACK], F32, "gain")
-        nc.sync.dma_start(gain[:], gn.rearrange("(p t) o -> p (t o)", t=PACK))
-        l_two = load_list(two, "l_two")
-        l_n1 = load_list(n1, "l_n1")
         xw_tab = new([P, TABLE], U32, "xw_tab")
         nc.sync.dma_start(xw_tab[:].bitcast(I32), words_of(x_words))
+        l_two = load_list(two, "l_two")
+        w_raw = [reuse.tile([P, S], U32, name=f"w_raw{w}", offset=(5 - 4 * w) * 1024) for w in range(2)]
+        w_dealt = new([P, 2, S], U32, "w_dealt")
+        for w, words in enumerate((w1_words, w2_words)):
+            nc.sync.dma_start(w_raw[w][:].bitcast(I32), words_of(words))
+        gain = new([P, PACK], F32, "gain")
+        nc.sync.dma_start(gain[:], gn.rearrange("(p t) o -> p (t o)", t=PACK))
+        l_n1 = load_list(n1, "l_n1")
         l_n2 = load_list(n2, "l_n2")
         l_n3 = load_list(n3, "l_n3")
         l_n4 = load_list(n4, "l_n4")
+        ws_raw = new([P, S], U8, "ws_raw")
+        nc.gpsimd.memset(ws_raw[:].bitcast(I32), 0)
+        for w, scales in enumerate((w1_scales, w2_scales)):
+            for q in range(4):
+                nc.gpsimd.dma_start(
+                    ws_raw[32 * q + 4 * w : 32 * q + 4 * w + 4, :].bitcast(I32), scales[0, 4 * q : 4 * q + 4, :].bitcast(I32)
+                )
 
         key_plane = new([P, S], U8, "key_plane")
         nc.vector.memset(key_plane[:].bitcast(I32), 0)
-        ex_win = [new([P, S + PAD], F32, f"ex_win{t}") for t in range(PACK)]
         hh_win = [new([P, S + PAD], F32, f"hh_win{t}") for t in range(PACK)]
-        for win in ex_win + hh_win:
+        for win in hh_win:
             nc.vector.memset(win[:, S:], 0.0)
 
         ds_got = new([P, S], U8, "ds_got")
@@ -94,20 +105,19 @@ def tile_picked_kmixlsehop_none_po_kernel(
         deal_bytes(ds_dealt[:], ds_got[:])
         for q in range(4):
             nc.scalar.dma_start(key_plane[32 * q : 32 * q + 4, :].bitcast(I32), ds_dealt[32 * q : 32 * q + 32 : 8, :].bitcast(I32))
-        tok_plane = new([P, S], U8, "tok_plane", tag="scales")
-        nc.vector.tensor_copy(out=tok_plane[:], in_=xs_tab[:].indirect(l_offs[:]))
-        dw_got = new([P, S], U32, "dw_got", tag="ds_got")
+        dw_got = new([P, S], U32, "dw_got", tag="scales")
         nc.vector.tensor_copy(out=dw_got[:], in_=dw_tab[:].indirect(l_k1[:]))
         key_words = new([P, S], U32, "key_words")
         deal_words(nc.vector.tensor_copy, key_words[:], dw_got[:])
+        tok_plane = new([P, S], U8, "tok_plane", tag="scales")
+        nc.vector.tensor_copy(out=tok_plane[:], in_=xs_tab[:].indirect(l_offs[:]))
         tok_words = new([P, S], U32, "tok_words")
         nc.vector.tensor_copy(out=tok_words[:], in_=xw_tab[:].indirect(l_offs[:]))
 
-        w_raw = new([P, 2, S], U32, "w_raw", tag="table")
-        w_dealt = new([P, 2, S], U32, "w_dealt")
-        for w, words in enumerate((w1_words, w2_words)):
-            nc.sync.dma_start(w_raw[:, w, :].bitcast(I32), words_of(words))
 
+        for w in range(2):
+            deal_words(nc.scalar.copy, w_dealt[:, w, :], w_raw[w][:])
+        ex_win = [reuse.tile([P, S], F32, name=f"ex_win{t}", offset=t * 2048) for t in range(PACK)]
         score = [ps.tile([P, S], F32, name=f"score{t}", tag=f"bank{t}") for t in range(PACK)]
         for t in range(PACK):
             nc.tensor.matmul_mx(
@@ -115,38 +125,32 @@ def tile_picked_kmixlsehop_none_po_kernel(
                 rhs=tok_words[:].bitcast(FP8X4), rhs_scale=tok_plane[:], start=True, stop=True,
             )
         for t in range(PACK):
-            nc.scalar.activation(out=ex_win[t][:, :S], in_=score[t][:], func=ACT.Exp, scale=0.0625)
+            nc.scalar.activation(out=ex_win[t][:], in_=score[t][:], func=ACT.Exp, scale=0.0625)
 
-        neg_gain = new([P, PACK], F32, "neg_gain")
-        nc.vector.tensor_scalar(out=neg_gain[:], in0=gain[:], scalar1=-0.0625, scalar2=None, op0=ALU.mult)
         two_words = new([P, S], U32, "two_words")
         nc.vector.tensor_copy(out=two_words[:], in_=xw_tab[:].indirect(l_two[:]))
-        two_plane = new([P, S], U8, "two_plane", tag="scales")
-        nc.vector.tensor_copy(out=two_plane[:], in_=xs_tab[:].indirect(l_two[:]))
-        ws_raw = new([P, S], U8, "ws_raw", tag="xs_tab")
-        nc.vector.memset(ws_raw[:].bitcast(I32), 0)
-        for w, scales in enumerate((w1_scales, w2_scales)):
-            for q in range(4):
-                nc.sync.dma_start(
-                    ws_raw[32 * q + 4 * w : 32 * q + 4 * w + 4, :].bitcast(I32), scales[0, 4 * q : 4 * q + 4, :].bitcast(I32)
-                )
 
-
+        neg_gain = new([P, PACK], F32, "neg_gain", tag="tok_words")
+        nc.scalar.activation(out=neg_gain[:], in_=gain[:], func=ACT.Copy, scale=-0.0625)
         gs_win = [new([P, S], F32, f"gs_win{t}") for t in range(PACK)]
         for t in range(PACK):
             nc.scalar.activation(out=gs_win[t][:], in_=score[t][:], func=ACT.Copy, scale=neg_gain[:, t : t + 1])
 
         ex = [new([P, S], F32, f"ex{t}") for t in range(PACK)]
         pair = [new([P, S], F32, f"pair{t}") for t in range(PACK)]
+        nc.vector.tensor_copy(out=ex[0][:], in_=ex_win[0][:])
+        for t in range(1, PACK):
+            nc.sync.dma_start(ex[t][:], ex_win[t][:])
+        two_plane = new([P, S], U8, "two_plane", tag="scales")
         for t in range(PACK):
-            nc.vector.tensor_copy(out=ex[t][:], in_=ex_win[t][:, :S])
-            if t > 0:
-                nc.vector.tensor_tensor(out=pair[t - 1][:], in0=ex_win[t - 1][:].indirect(l_n1[:]), in1=ex[t - 1][:], op=ALU.add)
-        nc.vector.tensor_tensor(out=pair[3][:], in0=ex_win[3][:].indirect(l_n1[:]), in1=ex[3][:], op=ALU.add)
+            for a in range(2):
+                nc.vector.tensor_tensor(
+                    out=pair[t][:, cols(a)], in0=ex_win[t][:].indirect(half_of(l_n1, a)), in1=ex[t][:, cols(a)], op=ALU.add
+                )
+            if t == 0:
+                nc.vector.tensor_copy(out=two_plane[:], in_=xs_tab[:].indirect(l_two[:]))
 
-        for w in range(2):
-            deal_words(nc.vector.tensor_copy, w_dealt[:, w, :], w_raw[:, w, :])
-        w_plane = new([P, S], U8, "w_plane")
+        w_plane = new([P, S], U8, "w_plane", tag="ex2")
         deal_bytes(w_plane[:], ws_raw[:])
 
         def project_two(bank, t, a):
@@ -161,23 +165,28 @@ def tile_picked_kmixlsehop_none_po_kernel(
                 project_two(hbank[a][t], t, a)
 
         lse = [new([P, S], F32, f"lse{t}") for t in range(PACK)]
-        gs_got = [[new([P, HALF], F32, f"gs_got{a}_{t}") for t in range(PACK)] for a in range(2)]
-        z_rows = [new([P, PACK, HALF], BF16, f"z_rows{a}") for a in range(2)]
+        gs_first = new([P, 2, HALF], F32, "gs_first", tag="ex3")
+        gs_got = [
+            [gs_first[:, t, :] if a == 0 and t < 2 else new([P, HALF], F32, f"gs_got{a}_{t}")[:] for t in range(PACK)]
+            for a in range(2)
+        ]
 
         def fetch_gs(a, t):
-            nc.scalar.activation(out=gs_got[a][t][:], in_=gs_win[t][:].indirect(half_of(l_n2, a)), func=ACT.Copy)
+            if a == 0 and t < 2:
+                nc.vector.tensor_copy(out=gs_got[a][t], in_=gs_win[t][:].indirect(half_of(l_n2, a)))
+            else:
+                nc.scalar.activation(out=gs_got[a][t], in_=gs_win[t][:].indirect(half_of(l_n2, a)), func=ACT.Copy)
 
-        def make_z(a, t):
+        def make_z(z_rows, a, t):
             nc.vector.scalar_tensor_tensor(
-                out=z_rows[a][:, t, :], in0=lse[t][:, cols(a)], scalar=gain[:, t : t + 1], in1=gs_got[a][t][:],
+                out=z_rows[:, t, :], in0=lse[t][:, cols(a)], scalar=gain[:, t : t + 1], in1=gs_got[a][t],
                 op0=ALU.mult, op1=ALU.add,
             )
 
-        h_sb = [new([P, S], F32, f"h_sb{t}") for t in range(PACK)]
 
-        def second_product(a):
+        def second_product(z_rows, a):
             z_woven = new([P, HALF, PACK], BF16, f"z_woven{a}")
-            weave(z_woven[:], z_rows[a][:])
+            weave(nc.vector.tensor_copy, z_woven[:], z_rows[:])
             z_words = new([P, HALF], U32, f"z_words{a}")
             z_plane = new([P, HALF], U8, f"z_plane{a}")
             nc.vector.quantize_mx(out=z_words[:].bitcast(FP8X4), scales=z_plane[:], in_=z_woven[:].rearrange("p j t -> p (j t)"))
@@ -187,22 +196,33 @@ def tile_picked_kmixlsehop_none_po_kernel(
                     rhs=z_words[:].bitcast(FP8X4), rhs_scale=z_plane[:], start=False, stop=True,
                 )
 
-        def empty_h(a, t):
+        def empty_half(a, t):
             nc.scalar.activation(out=hh_win[t][:, cols(a)], in_=hbank[a][t][:], func=ACT.Copy, scale=0.5)
+
+        def empty_whole(a, t):
             nc.scalar.copy(out=h_sb[t][:, cols(a)], in_=hbank[a][t][:])
+
+        def double(a, t):
+            nc.vector.tensor_scalar(out=h_sb[t][:, cols(a)], in0=hh_win[t][:, cols(a)], scalar1=2.0, scalar2=None, op0=ALU.mult)
 
         for t in range(PACK):
             nc.scalar.activation(out=lse[t][:], in_=pair[t][:], func=ACT.Ln)
-            fetch_gs(0, t)
-            make_z(0, t)
+        for a in range(2):
+            for t in range(PACK):
+                fetch_gs(a, t)
+        for a in range(2):
+            z_rows = new([P, PACK, HALF], BF16, f"z_rows{a}", tag="z_woven0" if a else "")
+            for t in range(PACK):
+                make_z(z_rows, a, t)
+            second_product(z_rows, a)
+        h_late = new([P, 2, S], F32, "h_late", tag="z_woven1")
+        h_sb = [new([P, S], F32, "h_sb0")[:], new([P, S], F32, "h_sb1")[:], h_late[:, 0, :], h_late[:, 1, :]]
         for t in range(PACK):
-            fetch_gs(1, t)
-        second_product(0)
-        for t in range(PACK):
-            make_z(1, t)
-        second_product(1)
-        for t in range(PACK):
-            empty_h(0, t)
+            empty_half(0, t)
+            if t < 2:
+                empty_whole(0, t)
+            else:
+                double(0, t)
 
         st = [new([P, S], F32, f"st{t}") for t in range(PACK)]
         st_got = [[new([P, HALF], F32, f"st_got{a}_{t}") for t in range(PACK)] for a in range(2)]
@@ -210,27 +230,34 @@ def tile_picked_kmixlsehop_none_po_kernel(
         y_rows = out_0.rearrange("(p t) j -> p t j", t=PACK)
         y_plane = new([P, S], U8, "y_plane")
 
-        def hop(a, t):
+        def fetch_st(a, t):
             nc.scalar.activation(out=st_got[a][t][:], in_=st[t][:].indirect(half_of(l_n4, a)), func=ACT.Copy)
+
+        def hop(a, t):
             nc.vector.tensor_tensor(out=y[a][:, t, :], in0=st[t][:, cols(a)], in1=st_got[a][t][:], op=ALU.subtract)
             nc.sync.dma_start(y_rows[:, t, cols(a)], y[a][:, t, :])
 
         def planes(a):
             y_woven = new([P, HALF, PACK], BF16, f"y_woven{a}")
-            weave(y_woven[:], y[a][:])
+            weave(nc.vector.tensor_copy if a else nc.scalar.copy, y_woven[:], y[a][:])
             y_words = new([P, HALF], U32, f"y_words{a}")
             nc.vector.quantize_mx(out=y_words[:].bitcast(FP8X4), scales=y_plane[:, cols(a)], in_=y_woven[:].rearrange("p j t -> p (j t)"))
             nc.sync.dma_start(words_of(out_1)[:, cols(a)], y_words[:].bitcast(I32))
 
         for t in range(PACK):
-            empty_h(1, t)
-            nc.vector.tensor_tensor(out=st[t][:], in0=hh_win[t][:].indirect(l_n3[:]), in1=h_sb[t][:], op=ALU.add)
-        for t in range(PACK):
-            hop(0, t)
-        planes(0)
-        for t in range(PACK):
-            hop(1, t)
+            empty_half(1, t)
+            if t == 0:
+                double(1, t)
+            else:
+                empty_whole(1, t)
+            nc.vector.tensor_tensor(out=st[t][:], in0=hh_win[t][:].indirect(l_n3[:]), in1=h_sb[t], op=ALU.add)
+        for a, t in ((0, 0), (1, 0), (0, 1), (1, 1), (0, 2), (1, 2), (0, 3), (1, 3)):
+            fetch_st(a, t)
+        for a in range(2):
+            for t in range(PACK):
+                hop(a, t)
         planes(1)
+        planes(0)
         for q in range(4):
             queue = nc.scalar if q % 2 else nc.sync
             queue.dma_start(out_2[0, 4 * q : 4 * q + 4, :].bitcast(I32), y_plane[32 * q : 32 * q + 4, :].bitcast(I32))

@@ -51,7 +51,6 @@ def tile_picked_kmixlsehop_none_po_kernel(
     with ExitStack() as ctx:
         lists = ctx.enter_context(tc.tile_pool(name="lists", bufs=1))
         sb = ctx.enter_context(tc.tile_pool(name="sb", bufs=1))
-        reuse = ctx.enter_context(tc.tile_pool(name="reuse", bufs=1))
         ps = ctx.enter_context(tc.psum_pool(name="ps", bufs=1))
 
         def load_list(dram, name):
@@ -75,10 +74,6 @@ def tile_picked_kmixlsehop_none_po_kernel(
         xw_tab = new([P, TABLE], U32, "xw_tab")
         nc.sync.dma_start(xw_tab[:].bitcast(I32), words_of(x_words))
         l_two = load_list(two, "l_two")
-        w_raw = [reuse.tile([P, S], U32, name=f"w_raw{w}", offset=(5 - 4 * w) * 1024) for w in range(2)]
-        w_dealt = new([P, 2, S], U32, "w_dealt")
-        for w, words in enumerate((w1_words, w2_words)):
-            nc.sync.dma_start(w_raw[w][:].bitcast(I32), words_of(words))
         gain = new([P, PACK], F32, "gain")
         nc.sync.dma_start(gain[:], gn.rearrange("(p t) o -> p (t o)", t=PACK))
         l_n1 = load_list(n1, "l_n1")
@@ -95,8 +90,9 @@ def tile_picked_kmixlsehop_none_po_kernel(
 
         key_plane = new([P, S], U8, "key_plane")
         nc.vector.memset(key_plane[:].bitcast(I32), 0)
+        ex_win = [new([P, S + PAD], F32, f"ex_win{t}") for t in range(PACK)]
         hh_win = [new([P, S + PAD], F32, f"hh_win{t}") for t in range(PACK)]
-        for win in hh_win:
+        for win in ex_win + hh_win:
             nc.vector.memset(win[:, S:], 0.0)
 
         ds_got = new([P, S], U8, "ds_got")
@@ -105,19 +101,20 @@ def tile_picked_kmixlsehop_none_po_kernel(
         deal_bytes(ds_dealt[:], ds_got[:])
         for q in range(4):
             nc.scalar.dma_start(key_plane[32 * q : 32 * q + 4, :].bitcast(I32), ds_dealt[32 * q : 32 * q + 32 : 8, :].bitcast(I32))
-        dw_got = new([P, S], U32, "dw_got", tag="scales")
+        tok_plane = new([P, S], U8, "tok_plane", tag="scales")
+        nc.vector.tensor_copy(out=tok_plane[:], in_=xs_tab[:].indirect(l_offs[:]))
+        dw_got = new([P, S], U32, "dw_got", tag="ds_got")
         nc.vector.tensor_copy(out=dw_got[:], in_=dw_tab[:].indirect(l_k1[:]))
         key_words = new([P, S], U32, "key_words")
         deal_words(nc.vector.tensor_copy, key_words[:], dw_got[:])
-        tok_plane = new([P, S], U8, "tok_plane", tag="scales")
-        nc.vector.tensor_copy(out=tok_plane[:], in_=xs_tab[:].indirect(l_offs[:]))
         tok_words = new([P, S], U32, "tok_words")
         nc.vector.tensor_copy(out=tok_words[:], in_=xw_tab[:].indirect(l_offs[:]))
 
 
-        for w in range(2):
-            deal_words(nc.scalar.copy, w_dealt[:, w, :], w_raw[w][:])
-        ex_win = [reuse.tile([P, S], F32, name=f"ex_win{t}", offset=t * 2048) for t in range(PACK)]
+        w_raw = new([P, 2, S], U32, "w_raw", tag="table")
+        for w, words in enumerate((w1_words, w2_words)):
+            nc.sync.dma_start(w_raw[:, w, :].bitcast(I32), words_of(words))
+
         score = [ps.tile([P, S], F32, name=f"score{t}", tag=f"bank{t}") for t in range(PACK)]
         for t in range(PACK):
             nc.tensor.matmul_mx(
@@ -125,12 +122,12 @@ def tile_picked_kmixlsehop_none_po_kernel(
                 rhs=tok_words[:].bitcast(FP8X4), rhs_scale=tok_plane[:], start=True, stop=True,
             )
         for t in range(PACK):
-            nc.scalar.activation(out=ex_win[t][:], in_=score[t][:], func=ACT.Exp, scale=0.0625)
+            nc.scalar.activation(out=ex_win[t][:, :S], in_=score[t][:], func=ACT.Exp, scale=0.0625)
 
         two_words = new([P, S], U32, "two_words")
         nc.vector.tensor_copy(out=two_words[:], in_=xw_tab[:].indirect(l_two[:]))
 
-        neg_gain = new([P, PACK], F32, "neg_gain", tag="tok_words")
+        neg_gain = new([P, PACK], F32, "neg_gain", tag="ds_got")
         nc.scalar.activation(out=neg_gain[:], in_=gain[:], func=ACT.Copy, scale=-0.0625)
         gs_win = [new([P, S], F32, f"gs_win{t}") for t in range(PACK)]
         for t in range(PACK):
@@ -138,18 +135,18 @@ def tile_picked_kmixlsehop_none_po_kernel(
 
         ex = [new([P, S], F32, f"ex{t}") for t in range(PACK)]
         pair = [new([P, S], F32, f"pair{t}") for t in range(PACK)]
-        nc.vector.tensor_copy(out=ex[0][:], in_=ex_win[0][:])
+        nc.vector.tensor_copy(out=ex[0][:], in_=ex_win[0][:, :S])
         for t in range(1, PACK):
-            nc.sync.dma_start(ex[t][:], ex_win[t][:])
+            nc.sync.dma_start(ex[t][:], ex_win[t][:, :S])
         two_plane = new([P, S], U8, "two_plane", tag="scales")
         for t in range(PACK):
-            for a in range(2):
-                nc.vector.tensor_tensor(
-                    out=pair[t][:, cols(a)], in0=ex_win[t][:].indirect(half_of(l_n1, a)), in1=ex[t][:, cols(a)], op=ALU.add
-                )
+            nc.vector.tensor_tensor(out=pair[t][:], in0=ex_win[t][:].indirect(l_n1[:]), in1=ex[t][:], op=ALU.add)
             if t == 0:
                 nc.vector.tensor_copy(out=two_plane[:], in_=xs_tab[:].indirect(l_two[:]))
 
+        w_dealt = new([P, 2, S], U32, "w_dealt")
+        for w in range(2):
+            deal_words(nc.vector.tensor_copy, w_dealt[:, w, :], w_raw[:, w, :])
         w_plane = new([P, S], U8, "w_plane", tag="ex2")
         deal_bytes(w_plane[:], ws_raw[:])
 
@@ -165,14 +162,12 @@ def tile_picked_kmixlsehop_none_po_kernel(
                 project_two(hbank[a][t], t, a)
 
         lse = [new([P, S], F32, f"lse{t}") for t in range(PACK)]
-        gs_first = new([P, 2, HALF], F32, "gs_first", tag="ex3")
         gs_got = [
-            [gs_first[:, t, :] if a == 0 and t < 2 else new([P, HALF], F32, f"gs_got{a}_{t}")[:] for t in range(PACK)]
-            for a in range(2)
+            [new([P, HALF], F32, f"gs_got{a}_{t}", tag="ex3" if a + t == 0 else "")[:] for t in range(PACK)] for a in range(2)
         ]
 
         def fetch_gs(a, t):
-            if a == 0 and t < 2:
+            if a + t == 0:
                 nc.vector.tensor_copy(out=gs_got[a][t], in_=gs_win[t][:].indirect(half_of(l_n2, a)))
             else:
                 nc.scalar.activation(out=gs_got[a][t], in_=gs_win[t][:].indirect(half_of(l_n2, a)), func=ACT.Copy)
@@ -211,18 +206,16 @@ def tile_picked_kmixlsehop_none_po_kernel(
             for t in range(PACK):
                 fetch_gs(a, t)
         for a in range(2):
-            z_rows = new([P, PACK, HALF], BF16, f"z_rows{a}", tag="z_woven0" if a else "")
+            z_rows = new([P, PACK, HALF], BF16, f"z_rows{a}")
             for t in range(PACK):
                 make_z(z_rows, a, t)
             second_product(z_rows, a)
-        h_late = new([P, 2, S], F32, "h_late", tag="z_woven1")
-        h_sb = [new([P, S], F32, "h_sb0")[:], new([P, S], F32, "h_sb1")[:], h_late[:, 0, :], h_late[:, 1, :]]
+        h_sb = [new([P, S], F32, "h_sb0"), new([P, S], F32, "h_sb1"), new([P, S], F32, "h_sb2", tag="z_woven1")]
         for t in range(PACK):
             empty_half(0, t)
             if t < 2:
                 empty_whole(0, t)
-            else:
-                double(0, t)
+        double(0, 2)
 
         st = [new([P, S], F32, f"st{t}") for t in range(PACK)]
         st_got = [[new([P, HALF], F32, f"st_got{a}_{t}") for t in range(PACK)] for a in range(2)]
@@ -244,13 +237,17 @@ def tile_picked_kmixlsehop_none_po_kernel(
             nc.vector.quantize_mx(out=y_words[:].bitcast(FP8X4), scales=y_plane[:, cols(a)], in_=y_woven[:].rearrange("p j t -> p (j t)"))
             nc.sync.dma_start(words_of(out_1)[:, cols(a)], y_words[:].bitcast(I32))
 
-        for t in range(PACK):
+        for t in range(PACK - 1):
             empty_half(1, t)
             if t == 0:
                 double(1, t)
             else:
                 empty_whole(1, t)
-            nc.vector.tensor_tensor(out=st[t][:], in0=hh_win[t][:].indirect(l_n3[:]), in1=h_sb[t], op=ALU.add)
+            nc.vector.tensor_tensor(out=st[t][:], in0=hh_win[t][:].indirect(l_n3[:]), in1=h_sb[t][:], op=ALU.add)
+        empty_half(1, 3)
+        hh_got = new([P, S], F32, "hh_got")
+        nc.scalar.activation(out=hh_got[:], in_=hh_win[3][:].indirect(l_n3[:]), func=ACT.Copy)
+        nc.vector.scalar_tensor_tensor(out=st[3][:], in0=hh_win[3][:, :S], scalar=2.0, in1=hh_got[:], op0=ALU.mult, op1=ALU.add)
         for a, t in ((0, 0), (1, 0), (0, 1), (1, 1), (0, 2), (1, 2), (0, 3), (1, 3)):
             fetch_st(a, t)
         for a in range(2):

@@ -74,12 +74,12 @@ def tile_picked_kmixlsehop_none_po_kernel(
         xw_tab = new([P, TABLE], U32, "xw_tab")
         nc.sync.dma_start(xw_tab[:].bitcast(I32), words_of(x_words))
         l_two = load_list(two, "l_two")
-        gain = new([P, PACK], F32, "gain")
-        nc.sync.dma_start(gain[:], gn.rearrange("(p t) o -> p (t o)", t=PACK))
         l_n1 = load_list(n1, "l_n1")
         l_n2 = load_list(n2, "l_n2")
         l_n3 = load_list(n3, "l_n3")
         l_n4 = load_list(n4, "l_n4")
+        gain = new([P, PACK], F32, "gain")
+        nc.gpsimd.dma_start(gain[:], gn.rearrange("(p t) o -> p (t o)", t=PACK))
         ws_raw = new([P, S], U8, "ws_raw")
         nc.gpsimd.memset(ws_raw[:].bitcast(I32), 0)
         for w, scales in enumerate((w1_scales, w2_scales)):
@@ -101,14 +101,17 @@ def tile_picked_kmixlsehop_none_po_kernel(
         deal_bytes(ds_dealt[:], ds_got[:])
         for q in range(4):
             nc.scalar.dma_start(key_plane[32 * q : 32 * q + 4, :].bitcast(I32), ds_dealt[32 * q : 32 * q + 32 : 8, :].bitcast(I32))
+        neg_gain = new([P, PACK], F32, "neg_gain")
+        nc.scalar.activation(out=neg_gain[:], in_=gain[:], func=ACT.Copy, scale=-0.0625)
         tok_plane = new([P, S], U8, "tok_plane", tag="scales")
         nc.vector.tensor_copy(out=tok_plane[:], in_=xs_tab[:].indirect(l_offs[:]))
         dw_got = new([P, S], U32, "dw_got", tag="ds_got")
         nc.vector.tensor_copy(out=dw_got[:], in_=dw_tab[:].indirect(l_k1[:]))
         key_words = new([P, S], U32, "key_words")
         deal_words(nc.vector.tensor_copy, key_words[:], dw_got[:])
-        tok_words = new([P, S], U32, "tok_words")
-        nc.vector.tensor_copy(out=tok_words[:], in_=xw_tab[:].indirect(l_offs[:]))
+        tok_words = [new([P, HALF], U32, f"tok_words{a}") for a in range(2)]
+        for a in range(2):
+            nc.vector.tensor_copy(out=tok_words[a][:], in_=xw_tab[:].indirect(half_of(l_offs, a)))
 
 
         w_raw = new([P, 2, S], U32, "w_raw", tag="table")
@@ -116,19 +119,18 @@ def tile_picked_kmixlsehop_none_po_kernel(
             nc.sync.dma_start(w_raw[:, w, :].bitcast(I32), words_of(words))
 
         score = [ps.tile([P, S], F32, name=f"score{t}", tag=f"bank{t}") for t in range(PACK)]
-        for t in range(PACK):
-            nc.tensor.matmul_mx(
-                out=score[t][:], lhsT=key_words[:, block(t)].bitcast(FP8X4), lhsT_scale=key_plane[:, block(t)],
-                rhs=tok_words[:].bitcast(FP8X4), rhs_scale=tok_plane[:], start=True, stop=True,
-            )
+        for a in range(2):
+            for t in range(PACK):
+                nc.tensor.matmul_mx(
+                    out=score[t][:, cols(a)], lhsT=key_words[:, block(t)].bitcast(FP8X4), lhsT_scale=key_plane[:, block(t)],
+                    rhs=tok_words[a][:].bitcast(FP8X4), rhs_scale=tok_plane[:, cols(a)], start=True, stop=True,
+                )
         for t in range(PACK):
             nc.scalar.activation(out=ex_win[t][:, :S], in_=score[t][:], func=ACT.Exp, scale=0.0625)
 
         two_words = new([P, S], U32, "two_words")
         nc.vector.tensor_copy(out=two_words[:], in_=xw_tab[:].indirect(l_two[:]))
 
-        neg_gain = new([P, PACK], F32, "neg_gain", tag="ds_got")
-        nc.scalar.activation(out=neg_gain[:], in_=gain[:], func=ACT.Copy, scale=-0.0625)
         gs_win = [new([P, S], F32, f"gs_win{t}") for t in range(PACK)]
         for t in range(PACK):
             nc.scalar.activation(out=gs_win[t][:], in_=score[t][:], func=ACT.Copy, scale=neg_gain[:, t : t + 1])
@@ -162,12 +164,14 @@ def tile_picked_kmixlsehop_none_po_kernel(
                 project_two(hbank[a][t], t, a)
 
         lse = [new([P, S], F32, f"lse{t}") for t in range(PACK)]
+        gs_first = new([P, 2, HALF], F32, "gs_first", tag="ex3")
         gs_got = [
-            [new([P, HALF], F32, f"gs_got{a}_{t}", tag="ex3" if a + t == 0 else "")[:] for t in range(PACK)] for a in range(2)
+            [gs_first[:, t, :] if a == 0 and t < 2 else new([P, HALF], F32, f"gs_got{a}_{t}")[:] for t in range(PACK)]
+            for a in range(2)
         ]
 
         def fetch_gs(a, t):
-            if a + t == 0:
+            if a == 0 and t < 2:
                 nc.vector.tensor_copy(out=gs_got[a][t], in_=gs_win[t][:].indirect(half_of(l_n2, a)))
             else:
                 nc.scalar.activation(out=gs_got[a][t], in_=gs_win[t][:].indirect(half_of(l_n2, a)), func=ACT.Copy)
@@ -210,12 +214,14 @@ def tile_picked_kmixlsehop_none_po_kernel(
             for t in range(PACK):
                 make_z(z_rows, a, t)
             second_product(z_rows, a)
-        h_sb = [new([P, S], F32, "h_sb0"), new([P, S], F32, "h_sb1"), new([P, S], F32, "h_sb2", tag="z_woven1")]
+        h_late = new([P, 2, S], F32, "h_late", tag="z_woven1")
+        h_sb = [new([P, S], F32, "h_sb0")[:], new([P, S], F32, "h_sb1")[:], h_late[:, 0, :], h_late[:, 1, :]]
         for t in range(PACK):
             empty_half(0, t)
             if t < 2:
                 empty_whole(0, t)
-        double(0, 2)
+            else:
+                double(0, t)
 
         st = [new([P, S], F32, f"st{t}") for t in range(PACK)]
         st_got = [[new([P, HALF], F32, f"st_got{a}_{t}") for t in range(PACK)] for a in range(2)]
@@ -237,17 +243,13 @@ def tile_picked_kmixlsehop_none_po_kernel(
             nc.vector.quantize_mx(out=y_words[:].bitcast(FP8X4), scales=y_plane[:, cols(a)], in_=y_woven[:].rearrange("p j t -> p (j t)"))
             nc.sync.dma_start(words_of(out_1)[:, cols(a)], y_words[:].bitcast(I32))
 
-        for t in range(PACK - 1):
+        for t in range(PACK):
             empty_half(1, t)
             if t == 0:
                 double(1, t)
             else:
                 empty_whole(1, t)
-            nc.vector.tensor_tensor(out=st[t][:], in0=hh_win[t][:].indirect(l_n3[:]), in1=h_sb[t][:], op=ALU.add)
-        empty_half(1, 3)
-        hh_got = new([P, S], F32, "hh_got")
-        nc.scalar.activation(out=hh_got[:], in_=hh_win[3][:].indirect(l_n3[:]), func=ACT.Copy)
-        nc.vector.scalar_tensor_tensor(out=st[3][:], in0=hh_win[3][:, :S], scalar=2.0, in1=hh_got[:], op0=ALU.mult, op1=ALU.add)
+            nc.vector.tensor_tensor(out=st[t][:], in0=hh_win[t][:].indirect(l_n3[:]), in1=h_sb[t], op=ALU.add)
         for a, t in ((0, 0), (1, 0), (0, 1), (1, 1), (0, 2), (1, 2), (0, 3), (1, 3)):
             fetch_st(a, t)
         for a in range(2):

from contextlib import ExitStack

import concourse.mybir as mybir

F32 = mybir.dt.float32
BF16 = mybir.dt.bfloat16
I32 = mybir.dt.int32
U32 = mybir.dt.uint32
U16 = mybir.dt.uint16
U8 = mybir.dt.uint8
FP8X4 = mybir.dt.float8_e4m3fn_x4
ACT = mybir.ActivationFunctionType
ALU = mybir.AluOpType

P = 128
PACK = 4
TABLE = 2048
S = 512
HALF = S // 2
PAD = 16
FLOPS = 3 * 2 * 512 * 512 * 512


def tile_picked_kmixlsehop_none_po_kernel(
    tc, x_words, x_scales, d_words, d_scales, gn, w1_words, w1_scales, w2_words, w2_scales,
    offs, k1, n1, n2, two, n3, n4, out_0, out_1, out_2,
):
    nc = tc.nc

    def words_of(dram):
        return dram[0].rearrange("p n t -> p (n t)").bitcast(I32)

    def half_of(lst, a):
        return lst[:, a * (HALF // 16) : (a + 1) * (HALF // 16)]

    def cols(a):
        return slice(a * HALF, (a + 1) * HALF)

    def block(t):
        return slice(t * P, (t + 1) * P)

    def deal_words(copy, dst, src):
        copy(out=dst.rearrange("p (t c i) -> p c t i", t=PACK, i=4), in_=src.rearrange("p (c i t) -> p c t i", t=PACK, i=4))

    def deal_bytes(dst, src):
        nc.vector.tensor_copy(out=dst.rearrange("p (t m) -> p t m", t=PACK), in_=src.rearrange("p (m t) -> p t m", t=PACK))

    def weave(copy, dst, src):
        copy(out=dst.rearrange("p (c i) t -> p c t i", i=4), in_=src.rearrange("p t (c i) -> p c t i", i=4))

    with ExitStack() as ctx:
        lists = ctx.enter_context(tc.tile_pool(name="lists", bufs=1))
        sb = ctx.enter_context(tc.tile_pool(name="sb", bufs=1))
        ps = ctx.enter_context(tc.psum_pool(name="ps", bufs=1))

        def load_list(dram, name):
            tl = lists.tile([P, S // 16], U16, name=name)
            nc.sync.dma_start(tl[:], dram)
            return tl

        def new(shape, dtype, name, tag=""):
            return sb.tile(shape, dtype, name=name, tag=tag or name, align_bytes=64)

        ds_tab = new([P, TABLE], U8, "ds_tab", tag="scales")
        xs_tab = new([P, TABLE], U8, "xs_tab")
        nc.vector.memset(xs_tab[:].bitcast(I32), 0)
        l_k1 = load_list(k1, "l_k1")
        nc.sync.dma_start(ds_tab[:].bitcast(I32), d_scales[0].bitcast(I32).unsqueeze(1).to_broadcast([16, 8, TABLE // 4]))
        l_offs = load_list(offs, "l_offs")
        for q in range(4):
            nc.scalar.dma_start(xs_tab[32 * q : 32 * q + 4, :].bitcast(I32), x_scales[0, 4 * q : 4 * q + 4, :].bitcast(I32))
        dw_tab = new([P, TABLE], U32, "dw_tab", tag="table")
        nc.sync.dma_start(dw_tab[:].bitcast(I32), words_of(d_words))
        xw_tab = new([P, TABLE], U32, "xw_tab")
        nc.sync.dma_start(xw_tab[:].bitcast(I32), words_of(x_words))
        l_two = load_list(two, "l_two")
        l_n1 = load_list(n1, "l_n1")
        l_n2 = load_list(n2, "l_n2")
        l_n3 = load_list(n3, "l_n3")
        l_n4 = load_list(n4, "l_n4")
        gain = new([P, PACK], F32, "gain")
        nc.gpsimd.dma_start(gain[:], gn.rearrange("(p t) o -> p (t o)", t=PACK))
        ws_raw = new([P, S], U8, "ws_raw")
        nc.gpsimd.memset(ws_raw[:].bitcast(I32), 0)
        for w, scales in enumerate((w1_scales, w2_scales)):
            for q in range(4):
                nc.gpsimd.dma_start(
                    ws_raw[32 * q + 4 * w : 32 * q + 4 * w + 4, :].bitcast(I32), scales[0, 4 * q : 4 * q + 4, :].bitcast(I32)
                )

        key_plane = new([P, S], U8, "key_plane")
        nc.vector.memset(key_plane[:].bitcast(I32), 0)
        ex_win = [new([P, S + PAD], F32, f"ex_win{t}") for t in range(PACK)]
        hh_win = [new([P, S + PAD], F32, f"hh_win{t}") for t in range(PACK)]
        for win in ex_win + hh_win:
            nc.vector.memset(win[:, S:], 0.0)

        ds_got = new([P, S], U8, "ds_got")
        nc.vector.tensor_copy(out=ds_got[:], in_=ds_tab[:].indirect(l_k1[:]))
        ds_dealt = new([P, S], U8, "ds_dealt")
        deal_bytes(ds_dealt[:], ds_got[:])
        for q in range(4):
            nc.scalar.dma_start(key_plane[32 * q : 32 * q + 4, :].bitcast(I32), ds_dealt[32 * q : 32 * q + 32 : 8, :].bitcast(I32))
        neg_gain = new([P, PACK], F32, "neg_gain")
        nc.scalar.activation(out=neg_gain[:], in_=gain[:], func=ACT.Copy, scale=-0.0625)
        tok_plane = new([P, S], U8, "tok_plane", tag="scales")
        nc.vector.tensor_copy(out=tok_plane[:], in_=xs_tab[:].indirect(l_offs[:]))
        dw_got = new([P, S], U32, "dw_got", tag="ds_got")
        nc.vector.tensor_copy(out=dw_got[:], in_=dw_tab[:].indirect(l_k1[:]))
        key_words = new([P, S], U32, "key_words")
        deal_words(nc.vector.tensor_copy, key_words[:], dw_got[:])
        tok_words = [new([P, HALF], U32, f"tok_words{a}") for a in range(2)]
        for a in range(2):
            nc.vector.tensor_copy(out=tok_words[a][:], in_=xw_tab[:].indirect(half_of(l_offs, a)))


        w_raw = new([P, 2, S], U32, "w_raw", tag="table")
        for w, words in enumerate((w1_words, w2_words)):
            nc.sync.dma_start(w_raw[:, w, :].bitcast(I32), words_of(words))

        score = [ps.tile([P, S], F32, name=f"score{t}", tag=f"bank{t}") for t in range(PACK)]
        for a in range(2):
            for t in range(PACK):
                nc.tensor.matmul_mx(
                    out=score[t][:, cols(a)], lhsT=key_words[:, block(t)].bitcast(FP8X4), lhsT_scale=key_plane[:, block(t)],
                    rhs=tok_words[a][:].bitcast(FP8X4), rhs_scale=tok_plane[:, cols(a)], start=True, stop=True,
                )
        for t in range(PACK):
            nc.scalar.activation(out=ex_win[t][:, :S], in_=score[t][:], func=ACT.Exp, scale=0.0625)

        two_words = new([P, S], U32, "two_words")
        nc.vector.tensor_copy(out=two_words[:], in_=xw_tab[:].indirect(l_two[:]))

        gs_win = [new([P, S], F32, f"gs_win{t}") for t in range(PACK)]
        for t in range(PACK):
            nc.scalar.activation(out=gs_win[t][:], in_=score[t][:], func=ACT.Copy, scale=neg_gain[:, t : t + 1])

        ex = [new([P, S], F32, f"ex{t}") for t in range(PACK)]
        pair = [new([P, S], F32, f"pair{t}") for t in range(PACK)]
        nc.vector.tensor_copy(out=ex[0][:], in_=ex_win[0][:, :S])
        for t in range(1, PACK):
            nc.sync.dma_start(ex[t][:], ex_win[t][:, :S])
        two_plane = new([P, S], U8, "two_plane", tag="scales")
        for t in range(PACK):
            nc.vector.tensor_tensor(out=pair[t][:], in0=ex_win[t][:].indirect(l_n1[:]), in1=ex[t][:], op=ALU.add)
            if t == 0:
                nc.vector.tensor_copy(out=two_plane[:], in_=xs_tab[:].indirect(l_two[:]))

        w_dealt = new([P, 2, S], U32, "w_dealt")
        for w in range(2):
            deal_words(nc.vector.tensor_copy, w_dealt[:, w, :], w_raw[:, w, :])
        w_plane = new([P, S], U8, "w_plane", tag="ex2")
        deal_bytes(w_plane[:], ws_raw[:])

        def project_two(bank, t, a):
            nc.tensor.matmul_mx(
                out=bank[:], lhsT=w_dealt[:, 1, block(t)].bitcast(FP8X4), lhsT_scale=w_plane[4:P, block(t)],
                rhs=two_words[:, cols(a)].bitcast(FP8X4), rhs_scale=two_plane[:, cols(a)], start=True, stop=False,
            )

        hbank = [[ps.tile([P, HALF], F32, name=f"h{a}_{t}", tag=f"bank{4 * (1 - a) + t}") for t in range(PACK)] for a in range(2)]
        for a in range(2):
            for t in range(PACK):
                project_two(hbank[a][t], t, a)

        lse = [new([P, S], F32, f"lse{t}") for t in range(PACK)]
        gs_first = new([P, 2, HALF], F32, "gs_first", tag="ex3")
        gs_got = [
            [gs_first[:, t, :] if a == 0 and t < 2 else new([P, HALF], F32, f"gs_got{a}_{t}")[:] for t in range(PACK)]
            for a in range(2)
        ]

        def fetch_gs(a, t):
            if a == 0 and t < 2:
                nc.vector.tensor_copy(out=gs_got[a][t], in_=gs_win[t][:].indirect(half_of(l_n2, a)))
            else:
                nc.scalar.activation(out=gs_got[a][t], in_=gs_win[t][:].indirect(half_of(l_n2, a)), func=ACT.Copy)

        def make_z(z_rows, a, t):
            nc.vector.scalar_tensor_tensor(
                out=z_rows[:, t, :], in0=lse[t][:, cols(a)], scalar=gain[:, t : t + 1], in1=gs_got[a][t],
                op0=ALU.mult, op1=ALU.add,
            )


        def second_product(z_rows, a):
            z_woven = new([P, HALF, PACK], BF16, f"z_woven{a}")
            weave(nc.vector.tensor_copy, z_woven[:], z_rows[:])
            z_words = new([P, HALF], U32, f"z_words{a}")
            z_plane = new([P, HALF], U8, f"z_plane{a}")
            nc.vector.quantize_mx(out=z_words[:].bitcast(FP8X4), scales=z_plane[:], in_=z_woven[:].rearrange("p j t -> p (j t)"))
            for t in range(PACK):
                nc.tensor.matmul_mx(
                    out=hbank[a][t][:], lhsT=w_dealt[:, 0, block(t)].bitcast(FP8X4), lhsT_scale=w_plane[:, block(t)],
                    rhs=z_words[:].bitcast(FP8X4), rhs_scale=z_plane[:], start=False, stop=True,
                )

        def empty_half(a, t):
            nc.scalar.activation(out=hh_win[t][:, cols(a)], in_=hbank[a][t][:], func=ACT.Copy, scale=0.5)

        def empty_whole(a, t):
            nc.scalar.copy(out=h_sb[t][:, cols(a)], in_=hbank[a][t][:])

        def double(a, t):
            nc.vector.tensor_scalar(out=h_sb[t][:, cols(a)], in0=hh_win[t][:, cols(a)], scalar1=2.0, scalar2=None, op0=ALU.mult)

        for t in range(PACK):
            nc.scalar.activation(out=lse[t][:], in_=pair[t][:], func=ACT.Ln)
        for a in range(2):
            for t in range(PACK):
                fetch_gs(a, t)
        for a in range(2):
            z_rows = new([P, PACK, HALF], BF16, f"z_rows{a}")
            for t in range(PACK):
                make_z(z_rows, a, t)
            second_product(z_rows, a)
        h_late = new([P, 2, S], F32, "h_late", tag="z_woven1")
        h_sb = [new([P, S], F32, "h_sb0")[:], new([P, S], F32, "h_sb1")[:], h_late[:, 0, :], h_late[:, 1, :]]
        for t in range(PACK):
            empty_half(0, t)
            if t < 2:
                empty_whole(0, t)
            else:
                double(0, t)

        st = [new([P, S], F32, f"st{t}") for t in range(PACK)]
        st_got = [[new([P, HALF], F32, f"st_got{a}_{t}") for t in range(PACK)] for a in range(2)]
        y = [new([P, PACK, HALF], F32, f"y{a}") for a in range(2)]
        y_rows = out_0.rearrange("(p t) j -> p t j", t=PACK)
        y_plane = new([P, S], U8, "y_plane")

        def fetch_st(a, t):
            nc.scalar.activation(out=st_got[a][t][:], in_=st[t][:].indirect(half_of(l_n4, a)), func=ACT.Copy)

        def hop(a, t):
            nc.vector.tensor_tensor(out=y[a][:, t, :], in0=st[t][:, cols(a)], in1=st_got[a][t][:], op=ALU.subtract)
            nc.sync.dma_start(y_rows[:, t, cols(a)], y[a][:, t, :])

        def planes(a):
            y_woven = new([P, HALF, PACK], BF16, f"y_woven{a}")
            weave(nc.vector.tensor_copy if a else nc.scalar.copy, y_woven[:], y[a][:])
            y_words = new([P, HALF], U32, f"y_words{a}")
            nc.vector.quantize_mx(out=y_words[:].bitcast(FP8X4), scales=y_plane[:, cols(a)], in_=y_woven[:].rearrange("p j t -> p (j t)"))
            nc.sync.dma_start(words_of(out_1)[:, cols(a)], y_words[:].bitcast(I32))

        for t in range(PACK):
            empty_half(1, t)
            if t == 0:
                double(1, t)
            else:
                empty_whole(1, t)
            nc.vector.tensor_tensor(out=st[t][:], in0=hh_win[t][:].indirect(l_n3[:]), in1=h_sb[t], op=ALU.add)
        for a, t in ((0, 0), (1, 0), (0, 1), (1, 1), (0, 2), (1, 2), (0, 3), (1, 3)):
            fetch_st(a, t)
        for a in range(2):
            for t in range(PACK):
                hop(a, t)
        planes(1)
        planes(0)
        for q in range(4):
            queue = nc.scalar if q % 2 else nc.sync
            queue.dma_start(out_2[0, 4 * q : 4 * q + 4, :].bitcast(I32), y_plane[32 * q : 32 * q + 4, :].bitcast(I32))
